import numpy as np
import ml_dtypes

BF16 = ml_dtypes.bfloat16


def bf(x):
    return np.asarray(x, np.float32).astype(BF16)


def f32(x):
    return np.asarray(x, np.float32)


def f64(x):
    return np.asarray(x).astype(np.float64)


def striped(idx):
    return np.tile(idx.reshape(-1, 16).T, (8, 1))


S, K, M, N = 512, 128, 256, 1024


def setup_inputs():
    return {"table": bf(np.random.standard_normal((K, S))), "w": bf(np.random.standard_normal((K, M)) / np.sqrt(K)), "offs": striped(np.random.permutation(np.tile(np.arange(S), 2))[:N])}


def reference(table, w, offs):
    idx = offs[:16].T.reshape(-1)
    x = f64(table)[:, idx]
    y = f64(w).T @ x
    return y

@@ -1,0 +1,39 @@
+import concourse.mybir as mybir
+
+BF16, F32, U16 = mybir.dt.bfloat16, mybir.dt.float32, mybir.dt.uint16
+
+P = 128
+S, M, N = 512, 256, 1024
+PIECE = 512
+PIECE_COLUMNS = PIECE // 16
+
+FLOPS = 2 * P * M * N
+
+
+def tile_gather_matmul_kernel(tc, table, w, offs, out):
+    nc = tc.nc
+    with (
+        tc.tile_pool(name="held", bufs=1) as held,
+        tc.tile_pool(name="staging", bufs=4) as staging,
+        tc.psum_pool(name="psum", bufs=4) as psum,
+    ):
+        offsets = held.tile([P, N // 16], U16, name="offsets")
+        nc.sync.dma_start(offsets[:], offs)
+        words = held.tile([P, S], BF16, name="words")
+        nc.scalar.dma_start(words[:], table)
+        weights = held.tile([P, M], BF16, name="weights")
+        nc.sync.dma_start(weights[:], w)
+
+        for piece in range(N // PIECE):
+            picked = words[:].indirect(offsets[:, piece * PIECE_COLUMNS : (piece + 1) * PIECE_COLUMNS])
+            for block in range(M // P):
+                bank = psum.tile([P, PIECE], F32, name="bank")
+                nc.tensor.matmul(bank[:], weights[:, block * P : (block + 1) * P], picked, start=True, stop=True)
+                staged = staging.tile([P, PIECE], F32, name="staged")
+                target = out[block * P : (block + 1) * P, piece * PIECE : (piece + 1) * PIECE]
+                if block % 2 == 0:
+                    nc.vector.tensor_copy(staged[:], bank[:])
+                    nc.sync.dma_start(target, staged[:])
+                else:
+                    nc.scalar.copy(staged[:], bank[:])
+                    nc.scalar.dma_start(target, staged[:])

@@ -7,6 +7,7 @@ S, M, N = 512, 256, 1024
 PIECE = 512
 PIECE_COLUMNS = PIECE // 16
 
+WARMING_MATMULS = 16
 FLOPS = 2 * P * M * N
 
 
@@ -23,6 +24,12 @@ def tile_gather_matmul_kernel(tc, table, w, offs, out):
         nc.scalar.dma_start(words[:], table)
         weights = held.tile([P, M], BF16, name="weights")
         nc.sync.dma_start(weights[:], w)
+
+        zeros = held.tile([P, P], BF16, name="zeros")
+        nc.vector.memset(zeros[:], 0.0)
+        unread = psum.tile([P, P], F32, name="unread")
+        for warming in range(WARMING_MATMULS):
+            nc.tensor.matmul(unread[:], zeros[:], zeros[:], start=True, stop=True)
 
         for piece in range(N // PIECE):
             picked = words[:].indirect(offsets[:, piece * PIECE_COLUMNS : (piece + 1) * PIECE_COLUMNS])

@@ -4,10 +4,9 @@ BF16, F32, U16 = mybir.dt.bfloat16, mybir.dt.float32, mybir.dt.uint16
 
 P = 128
 S, M, N = 512, 256, 1024
-PIECE = 512
+PIECE = 256
 PIECE_COLUMNS = PIECE // 16
 
-WARMING_MATMULS = 16
 FLOPS = 2 * P * M * N
 
 
@@ -15,8 +14,8 @@ def tile_gather_matmul_kernel(tc, table, w, offs, out):
     nc = tc.nc
     with (
         tc.tile_pool(name="held", bufs=1) as held,
-        tc.tile_pool(name="staging", bufs=4) as staging,
-        tc.psum_pool(name="psum", bufs=4) as psum,
+        tc.tile_pool(name="staging", bufs=8) as staging,
+        tc.psum_pool(name="psum", bufs=8) as psum,
     ):
         offsets = held.tile([P, N // 16], U16, name="offsets")
         nc.sync.dma_start(offsets[:], offs)
@@ -24,12 +23,6 @@ def tile_gather_matmul_kernel(tc, table, w, offs, out):
         nc.scalar.dma_start(words[:], table)
         weights = held.tile([P, M], BF16, name="weights")
         nc.sync.dma_start(weights[:], w)
-
-        zeros = held.tile([P, P], BF16, name="zeros")
-        nc.vector.memset(zeros[:], 0.0)
-        unread = psum.tile([P, P], F32, name="unread")
-        for warming in range(WARMING_MATMULS):
-            nc.tensor.matmul(unread[:], zeros[:], zeros[:], start=True, stop=True)
 
         for piece in range(N // PIECE):
             picked = words[:].indirect(offsets[:, piece * PIECE_COLUMNS : (piece + 1) * PIECE_COLUMNS])

@@ -31,9 +31,8 @@ def tile_gather_matmul_kernel(tc, table, w, offs, out):
                 nc.tensor.matmul(bank[:], weights[:, block * P : (block + 1) * P], picked, start=True, stop=True)
                 staged = staging.tile([P, PIECE], F32, name="staged")
                 target = out[block * P : (block + 1) * P, piece * PIECE : (piece + 1) * PIECE]
+                nc.vector.tensor_copy(staged[:], bank[:])
                 if block % 2 == 0:
-                    nc.vector.tensor_copy(staged[:], bank[:])
                     nc.sync.dma_start(target, staged[:])
                 else:
-                    nc.scalar.copy(staged[:], bank[:])
                     nc.scalar.dma_start(target, staged[:])

@@ -4,8 +4,9 @@ BF16, F32, U16 = mybir.dt.bfloat16, mybir.dt.float32, mybir.dt.uint16
 
 P = 128
 S, M, N = 512, 256, 1024
-PIECE = 256
-PIECE_COLUMNS = PIECE // 16
+PIECES = (256, 256, 256, 128, 128)
+assert sum(PIECES) == N
+PRODUCTS = len(PIECES) * (M // P)
 
 FLOPS = 2 * P * M * N
 
@@ -14,7 +15,7 @@ def tile_gather_matmul_kernel(tc, table, w, offs, out):
     nc = tc.nc
     with (
         tc.tile_pool(name="held", bufs=1) as held,
-        tc.tile_pool(name="staging", bufs=8) as staging,
+        tc.tile_pool(name="staging", bufs=PRODUCTS) as staging,
         tc.psum_pool(name="psum", bufs=8) as psum,
     ):
         offsets = held.tile([P, N // 16], U16, name="offsets")
@@ -24,15 +25,17 @@ def tile_gather_matmul_kernel(tc, table, w, offs, out):
         weights = held.tile([P, M], BF16, name="weights")
         nc.sync.dma_start(weights[:], w)
 
-        for piece in range(N // PIECE):
-            picked = words[:].indirect(offsets[:, piece * PIECE_COLUMNS : (piece + 1) * PIECE_COLUMNS])
+        first = 0
+        for width in PIECES:
+            picked = words[:].indirect(offsets[:, first // 16 : (first + width) // 16])
             for block in range(M // P):
-                bank = psum.tile([P, PIECE], F32, name="bank")
+                bank = psum.tile([P, width], F32, name="bank")
                 nc.tensor.matmul(bank[:], weights[:, block * P : (block + 1) * P], picked, start=True, stop=True)
-                staged = staging.tile([P, PIECE], F32, name="staged")
-                target = out[block * P : (block + 1) * P, piece * PIECE : (piece + 1) * PIECE]
+                staged = staging.tile([P, width], F32, name="staged")
+                target = out[block * P : (block + 1) * P, first : first + width]
                 nc.vector.tensor_copy(staged[:], bank[:])
                 if block % 2 == 0:
                     nc.sync.dma_start(target, staged[:])
                 else:
                     nc.scalar.dma_start(target, staged[:])
+            first += width

@@ -34,8 +34,5 @@ def tile_gather_matmul_kernel(tc, table, w, offs, out):
                 staged = staging.tile([P, width], F32, name="staged")
                 target = out[block * P : (block + 1) * P, first : first + width]
                 nc.vector.tensor_copy(staged[:], bank[:])
-                if block % 2 == 0:
-                    nc.sync.dma_start(target, staged[:])
-                else:
-                    nc.scalar.dma_start(target, staged[:])
+                nc.sync.dma_start(target, staged[:])
             first += width

@@ -4,7 +4,7 @@ BF16, F32, U16 = mybir.dt.bfloat16, mybir.dt.float32, mybir.dt.uint16
 
 P = 128
 S, M, N = 512, 256, 1024
-PIECES = (256, 256, 256, 128, 128)
+PIECES = (128, 128, 256, 256, 128, 128)
 assert sum(PIECES) == N
 PRODUCTS = len(PIECES) * (M // P)
 

@@ -18,12 +18,12 @@ def tile_gather_matmul_kernel(tc, table, w, offs, out):
         tc.tile_pool(name="staging", bufs=PRODUCTS) as staging,
         tc.psum_pool(name="psum", bufs=8) as psum,
     ):
+        words = held.tile([P, S], BF16, name="words")
+        nc.sync.dma_start(words[:], table)
+        weights = held.tile([P, M], BF16, name="weights")
+        nc.scalar.dma_start(weights[:], w)
         offsets = held.tile([P, N // 16], U16, name="offsets")
         nc.sync.dma_start(offsets[:], offs)
-        words = held.tile([P, S], BF16, name="words")
-        nc.scalar.dma_start(words[:], table)
-        weights = held.tile([P, M], BF16, name="weights")
-        nc.sync.dma_start(weights[:], w)
 
         first = 0
         for width in PIECES:

import concourse.mybir as mybir

BF16, F32, U16 = mybir.dt.bfloat16, mybir.dt.float32, mybir.dt.uint16

P = 128
S, M, N = 512, 256, 1024
PIECES = (128, 128, 256, 256, 128, 128)
assert sum(PIECES) == N
PRODUCTS = len(PIECES) * (M // P)

FLOPS = 2 * P * M * N


def tile_gather_matmul_kernel(tc, table, w, offs, out):
    nc = tc.nc
    with (
        tc.tile_pool(name="held", bufs=1) as held,
        tc.tile_pool(name="staging", bufs=PRODUCTS) as staging,
        tc.psum_pool(name="psum", bufs=8) as psum,
    ):
        words = held.tile([P, S], BF16, name="words")
        nc.sync.dma_start(words[:], table)
        weights = held.tile([P, M], BF16, name="weights")
        nc.scalar.dma_start(weights[:], w)
        offsets = held.tile([P, N // 16], U16, name="offsets")
        nc.sync.dma_start(offsets[:], offs)

        first = 0
        for width in PIECES:
            picked = words[:].indirect(offsets[:, first // 16 : (first + width) // 16])
            for block in range(M // P):
                bank = psum.tile([P, width], F32, name="bank")
                nc.tensor.matmul(bank[:], weights[:, block * P : (block + 1) * P], picked, start=True, stop=True)
                staged = staging.tile([P, width], F32, name="staged")
                target = out[block * P : (block + 1) * P, first : first + width]
                nc.vector.tensor_copy(staged[:], bank[:])
                nc.sync.dma_start(target, staged[:])
            first += width
